import numpy as np
import ml_dtypes


def mxq(x, axis, fmt="e4m3"):
    dtype, down = {"e4m3": (ml_dtypes.float8_e4m3fn, 7), "e5m2": (ml_dtypes.float8_e5m2, 14)}[fmt]
    v = np.moveaxis(np.asarray(x, np.float32).astype(ml_dtypes.bfloat16).astype(np.float64), axis, -1)
    blocks = v.reshape(v.shape[:-1] + (-1, 32))
    amax = np.abs(blocks).max(-1, keepdims=True)
    byte = np.maximum(np.where(amax > 0, np.frexp(amax)[1] - 1 + 127, 0) - down, 1)
    scale = np.exp2(byte - 127.0)
    codes = (blocks / scale).astype(np.float32).astype(dtype).astype(np.float64)
    return np.moveaxis((codes * scale).reshape(v.shape), -1, axis)


WIDE = False


def mx_kscale(k):
    if not WIDE:
        return np.ones(k)
    levels = np.array([10, -10, 5, -5, 0])
    if k % 512:
        return np.exp2(np.random.permutation(np.resize(levels, k // 32))).repeat(32)
    a = np.empty((k // 512, 16))
    for p in range(k // 512):
        a[p, :8] = np.random.permutation(np.resize(levels, 8))
        for g in range(8):
            far = levels[np.abs(levels - a[p, g]) >= 10]
            a[p, g + 8] = far[np.random.randint(len(far))]
    return np.exp2(a.ravel()).repeat(32)


def f64(x):
    return np.asarray(x).astype(np.float64)


def striped(idx):
    return np.tile(idx.reshape(-1, 16).T, (8, 1)).astype(np.uint16)


def unstriped(offs):
    return offs[:16].T.reshape(-1).astype(np.int64)


def pack_weight(w):
    k, n = w.shape
    w = f64(np.asarray(w, np.float32).astype(ml_dtypes.bfloat16)).reshape(k // 32, 32, n)
    amax = np.abs(w).max(1)
    byte = np.clip(np.where(amax > 0, np.frexp(amax)[1] - 1 + 127 - 7, 1), 1, 254)
    scaled = (w * np.exp2(127.0 - byte)[:, None, :]).reshape(k, n).astype(np.float32)
    words = np.ascontiguousarray(scaled.reshape(k // 512, 128, 4, n).transpose(0, 1, 3, 2)).astype(ml_dtypes.float8_e4m3fn).view(np.uint8)
    return words, np.ascontiguousarray(byte.astype(np.uint8).reshape(k // 512, 16, n))


def unpack_weight(words, scales):
    g, p, n, _ = words.shape
    vals = np.ascontiguousarray(words).view(ml_dtypes.float8_e4m3fn).astype(np.float64) * np.repeat(np.exp2(scales.astype(np.float64) - 127.0), 8, axis=1)[..., None]
    return vals.transpose(0, 1, 3, 2).reshape(g * 512, n)


K, T, S, N = 1024, 2048, 512, 256


def setup_inputs():
    n = np.random.standard_normal
    s = mx_kscale(K)[:, None]
    packed_xT = pack_weight(n((K, T)) * s)
    return {
        "x_words": packed_xT[0],
        "x_scales": packed_xT[1],
        "w1": (n((K, N)) / np.sqrt(K) / s).astype(np.float32),
        "inc": (np.random.uniform(0.2, 3.0, (N, S))).astype(np.float32),
        "disp": (np.random.uniform(1.0, 6.0, (N, 1))).astype(np.float32),
        "offs": striped(np.random.permutation(T)[:S]),
    }


def reference(x_words, x_scales, w1, inc, disp, offs):
    xq = unpack_weight(x_words, x_scales)[:, unstriped(offs)]
    y = mxq(f64(w1), 0, "e4m3").T @ xq
    rep = 1.3 * (np.log(np.exp(y) + 1.0))
    mu = rep * (0.2 * (np.pad(f64(inc), ((0, 0), (1, 0)))[:, :S]) + 0.5 * (np.pad(f64(inc), ((0, 0), (2, 0)))[:, :S]) + 0.3 * (np.pad(f64(inc), ((0, 0), (3, 0)))[:, :S]))
    rp = 0.4 * mu + 0.4 * (np.pad(mu, ((0, 0), (1, 0)))[:, :S]) + 0.2 * (np.pad(mu, ((0, 0), (2, 0)))[:, :S])
    return ((f64(inc) - rp) ** 2) / (rp + f64(disp) * ((rp) ** 2) + 0.1)

from contextlib import ExitStack

import concourse.mybir as mybir

K, T, S, N = 1024, 2048, 512, 256
FLOPS = 2 * K * S * N

F32 = mybir.dt.float32
BF16 = mybir.dt.bfloat16
I32 = mybir.dt.int32
U32 = mybir.dt.uint32
U16 = mybir.dt.uint16
U8 = mybir.dt.uint8
FP8X4 = mybir.dt.float8_e4m3fn_x4
ALU = mybir.AluOpType
ACT = mybir.ActivationFunctionType

P = 128
PACK = 4
PASSES = K // (P * PACK)
M_TILES = N // P
HALF = S // 2
PAD = 8
TINY = 2.0 ** -63


def tile_picked_yrenew_rep_p_kernel(tc, x_words, x_scales, w1, inc, disp, offs, out):
    nc = tc.nc
    with ExitStack() as ctx:
        keep = ctx.enter_context(tc.tile_pool(name="keep", bufs=1))
        psum = ctx.enter_context(tc.psum_pool(name="psum", bufs=1))

        def held(shape, dtype, name):
            return keep.tile(shape, dtype, name=name, align_bytes=64)

        offsets = keep.tile([P, S // 16], U16, name="offsets")
        scale_win = held([P, T], U8, "scale_win")
        scale_in = held([P, T], U8, "scale_in")
        warm = held([P, 3], F32, "warm")
        inc_sb = held([P, M_TILES, PAD + S], F32, "inc_sb")
        mu = held([P, M_TILES, PAD + S], F32, "mu")
        disp_sb = held([P, M_TILES, 1], F32, "disp_sb")

        nc.vector.memset(scale_win[:].bitcast(I32), 0)
        nc.vector.memset(warm[:, 0:1], 0.0)
        nc.scalar.activation(warm[:, 1:2], warm[:, 0:1], ACT.Sigmoid)
        nc.vector.memset(inc_sb[:, :, 0:PAD], 0.0)
        nc.vector.memset(mu[:, :, 0:PAD], 0.0)

        nc.sync.dma_start(offsets[:], offs)
        for q in range(4):
            nc.sync.dma_start(
                out=scale_in[32 * q : 32 * q + 4 * PASSES, :].bitcast(I32),
                in_=x_scales[:, 4 * q : 4 * q + 4, :].bitcast(I32),
            )
        for q in range(4):
            live = slice(32 * q, 32 * q + 4 * PASSES)
            nc.vector.tensor_copy(scale_win[live, :].bitcast(I32), scale_in[live, :].bitcast(I32))
        w_raw = []
        for g in range(PASSES):
            raw = held([P, PACK, N], F32, "w_raw%d" % g)
            nc.scalar.dma_start(out=raw[:], in_=w1[512 * g : 512 * (g + 1), :].rearrange("(p t) m -> p t m", t=PACK))
            w_raw.append(raw)
        word_win = []
        for g in range(PASSES):
            win = held([P, T], U32, "word_win%d" % g)
            nc.sync.dma_start(out=win[:].bitcast(I32), in_=x_words[g].rearrange("p c t -> p (c t)").bitcast(I32))
            word_win.append(win)
        nc.sync.dma_start(out=inc_sb[:, :, PAD:], in_=inc.rearrange("(a p) j -> p a j", p=P))
        with nc.allow_non_contiguous_dma(reason="one dispersion a partition"):
            nc.sync.dma_start(out=disp_sb[:], in_=disp.rearrange("(a p) o -> p a o", p=P))

        w_codes, w_scales = [], []
        for g in range(PASSES):
            grouped = held([P, N, PACK], BF16, "w_grouped%d" % g)
            nc.scalar.copy(
                grouped[:].rearrange("p (c i) t -> p c t i", i=4),
                w_raw[g][:].rearrange("p t (c i) -> p c t i", i=4),
            )
            codes = held([P, N], U32, "w_codes%d" % g)
            scales = held([P, N], U8, "w_scales%d" % g)
            nc.vector.quantize_mx(out=codes[:].bitcast(FP8X4), scales=scales[:], in_=grouped[:].rearrange("p m t -> p (m t)"))
            w_codes.append(codes)
            w_scales.append(scales)

        x_scale = held([P, S], U8, "x_scale")
        nc.vector.tensor_copy(x_scale[:], scale_win[:].indirect(offsets[:]))
        x_code0 = held([P, S], U32, "x_code0")
        nc.vector.tensor_copy(x_code0[:], word_win[0][:].indirect(offsets[:]))

        banks = {}
        for h in range(2):
            cols = slice(h * HALF, (h + 1) * HALF)
            for a in range(M_TILES):
                bank = psum.tile([P, 512], F32, name="y%d%d" % (h, a))
                banks[h, a] = bank
                rows = slice(a * P, (a + 1) * P)
                nc.tensor.matmul_mx(
                    out=bank[:, 0:HALF], lhsT=w_codes[0][:, rows].bitcast(FP8X4), lhsT_scale=w_scales[0][:, rows],
                    rhs=x_code0[:, cols].bitcast(FP8X4), rhs_scale=x_scale[:, cols], start=True, stop=False)
        sig = held([P, M_TILES, S], F32, "sig")
        for h in range(2):
            cols = slice(h * HALF, (h + 1) * HALF)
            x_code1 = held([P, HALF], U32, "x_code1_%d" % h)
            nc.vector.tensor_copy(x_code1[:], word_win[1][:].indirect(offsets[:, 16 * h : 16 * (h + 1)]))
            for a in range(M_TILES):
                rows = slice(a * P, (a + 1) * P)
                nc.tensor.matmul_mx(
                    out=banks[h, a][:, 0:HALF], lhsT=w_codes[1][:, rows].bitcast(FP8X4), lhsT_scale=w_scales[1][:, rows],
                    rhs=x_code1[:].bitcast(FP8X4), rhs_scale=x_scale[4:P, cols], start=False, stop=True)
                nc.scalar.activation(sig[:, a, cols], banks[h, a][:, 0:HALF], ACT.Sigmoid, scale=-1.0)

        part = held([P, M_TILES, S], F32, "part")
        force = held([P, M_TILES, S], F32, "force")
        nc.vector.scalar_tensor_tensor(
            out=part[:], in0=inc_sb[:, :, PAD - 1 : PAD - 1 + S], scalar=0.4, in1=inc_sb[:, :, PAD - 2 : PAD - 2 + S],
            op0=ALU.mult, op1=ALU.add)
        nc.vector.scalar_tensor_tensor(
            out=force[:], in0=inc_sb[:, :, PAD - 3 : PAD - 3 + S], scalar=0.6, in1=part[:], op0=ALU.mult, op1=ALU.add)

        names = ["lg", "sp", "pair", "rp", "lin", "diff", "var", "rs", "z", "res"]
        tl = {n: held([P, M_TILES, S], F32, n) for n in names}
        halves = [slice(h * HALF, (h + 1) * HALF) for h in range(2)]

        def at(t, h, shift=0):
            return t[:, :, PAD + h * HALF - shift : PAD + (h + 1) * HALF - shift]

        for h in range(2):
            for a in range(M_TILES):
                nc.scalar.activation(tl["lg"][:, a, halves[h]], sig[:, a, halves[h]], ACT.Ln, bias=TINY)
        nc.scalar.activation(warm[:, 2:3], tl["lg"][:, M_TILES - 1, S - 1 : S], ACT.Abs_reciprocal_sqrt, bias=0.1)
        for h in range(2):
            for a in range(M_TILES):
                nc.vector.scalar_tensor_tensor(
                    out=tl["sp"][:, a, halves[h]], in0=tl["lg"][:, a, halves[h]], scalar=-1.0, in1=banks[h, a][:, 0:HALF],
                    op0=ALU.mult, op1=ALU.max)
        for h in range(2):
            nc.vector.scalar_tensor_tensor(
                out=at(mu, h), in0=tl["sp"][:, :, halves[h]], scalar=1.3 * 0.5 * 0.4, in1=force[:, :, halves[h]],
                op0=ALU.mult, op1=ALU.mult)
        for h in range(2):
            nc.vector.tensor_tensor(tl["pair"][:, :, halves[h]], at(mu, h), at(mu, h, 1), ALU.add)
        for h in range(2):
            nc.vector.scalar_tensor_tensor(
                out=tl["rp"][:, :, halves[h]], in0=at(mu, h, 2), scalar=0.5, in1=tl["pair"][:, :, halves[h]],
                op0=ALU.mult, op1=ALU.add)
        for h in range(2):
            for a in range(M_TILES):
                nc.scalar.activation(tl["lin"][:, a, halves[h]], tl["rp"][:, a, halves[h]], ACT.Identity,
                                     bias=1.0, scale=disp_sb[:, a, :])
        for h in range(2):
            nc.vector.tensor_tensor(tl["diff"][:, :, halves[h]], at(inc_sb, h), tl["rp"][:, :, halves[h]], ALU.subtract)
            nc.vector.tensor_tensor(tl["var"][:, :, halves[h]], tl["lin"][:, :, halves[h]], tl["rp"][:, :, halves[h]], ALU.mult)
            nc.scalar.activation(tl["rs"][:, :, halves[h]], tl["var"][:, :, halves[h]], ACT.Abs_reciprocal_sqrt, bias=0.1)
        out_v = out.rearrange("(a p) j -> p a j", p=P)
        for h in range(2):
            for a in range(M_TILES):
                nc.vector.tensor_tensor(tl["z"][:, a, halves[h]], tl["diff"][:, a, halves[h]], tl["rs"][:, a, halves[h]], ALU.mult)
                nc.scalar.activation(tl["res"][:, a, halves[h]], tl["z"][:, a, halves[h]], ACT.Square)
                nc.sync.dma_start(out=out_v[:, a, halves[h]], in_=tl["res"][:, a, halves[h]])
